import numpy as np
CORES = [88,89,90,91,92,93,94,95,96,97,98,99,100,101,102,103]
N = 16
GROUPS = [[0,1,2,3],[4,5,6,7],[8,9,10,11],[12,13,14,15]]
def setup_inputs(rng):
    return {"x": rng.standard_normal((N, 128, 256), dtype=np.float32)}
def reference(x):
    y = np.empty((N, 128, 1024), x.dtype)
    for g in GROUPS:
        s = np.concatenate([x[r] for r in g], axis=1)
        for r in g:
            y[r] = s
    return {"y": y}

from concourse.bass import DstId, RemoteDMATransfer

W = 256
G = 4

SCRATCH = {
    "gather": ("sbuf", [128, G * W], "float32"),
}
SEMAPHORES = ["loaded", "sent", "arr0", "arr1", "arr2", "arr3", "st_hw", "st_sw"]

ALL_ENGINES = 0xFFFF


def rank_program(g, core, T, topo):
    rank = T.rank_of(core)
    if rank is None:
        return
    group = [grp for grp in T.tables["GROUPS"] if rank in grp][0]
    p = group.index(rank)
    peers = [q for q in range(len(group)) if q != p]

    def blk(t, q):
        return t[:, q * W:(q + 1) * W]

    g.sync.dma_start(blk(T.gather, p), T.x[:]).then_inc(T.sem.loaded, 16)
    g.scalar.dma_start(blk(T.y, p), T.x[:]).then_inc(T.sem.st_hw, 16)

    g.wait_ge(T.sem.loaded, 16)
    dst_ids = []
    for q in peers:
        rid, pid, _se = topo.addr(T.cores[group[q]])
        dst_ids.append(DstId(rid=rid, pnc=pid))
    g.remote_dma_fused(
        [RemoteDMATransfer(dst_ids=dst_ids, dma_engine_mask=ALL_ENGINES, remote_sem=T.sem["arr%d" % p],
                           srcs=[blk(T.gather, p)], dsts=[blk(T.gather, p) for _q in peers])],
        local_sem=T.sem.sent)

    queues = [(g.sync, T.sem.st_hw), (g.scalar, T.sem.st_hw), (g, T.sem.st_sw)]
    for (qu, done), q in zip(queues, peers):
        qu.wait_ge(T.sem["arr%d" % q], 16)
        qu.dma_start(blk(T.y, q), blk(T.gather, q)).then_inc(done, 16)

    g.wait_ge(T.sem.sent, 16)
    g.wait_ge(T.sem.st_sw, 16)
    g.wait_ge(T.sem.st_hw, 48)
